import numpy as np
import ml_dtypes


def mxq(x, axis, fmt="e4m3"):
    dtype, down = {"e4m3": (ml_dtypes.float8_e4m3fn, 7), "e5m2": (ml_dtypes.float8_e5m2, 14)}[fmt]
    v = np.moveaxis(np.asarray(x, np.float32).astype(ml_dtypes.bfloat16).astype(np.float64), axis, -1)
    blocks = v.reshape(v.shape[:-1] + (-1, 32))
    amax = np.abs(blocks).max(-1, keepdims=True)
    byte = np.maximum(np.where(amax > 0, np.frexp(amax)[1] - 1 + 127, 0) - down, 1)
    scale = np.exp2(byte - 127.0)
    codes = (blocks / scale).astype(np.float32).astype(dtype).astype(np.float64)
    return np.moveaxis((codes * scale).reshape(v.shape), -1, axis)


WIDE = False


def mx_kscale(k):
    if not WIDE:
        return np.ones(k)
    levels = np.array([10, -10, 5, -5, 0])
    if k % 512:
        return np.exp2(np.random.permutation(np.resize(levels, k // 32))).repeat(32)
    a = np.empty((k // 512, 16))
    for p in range(k // 512):
        a[p, :8] = np.random.permutation(np.resize(levels, 8))
        for g in range(8):
            far = levels[np.abs(levels - a[p, g]) >= 10]
            a[p, g + 8] = far[np.random.randint(len(far))]
    return np.exp2(a.ravel()).repeat(32)


def f64(x):
    return np.asarray(x).astype(np.float64)


def striped(idx):
    return np.tile(idx.reshape(-1, 16).T, (8, 1)).astype(np.uint16)


def unstriped(offs):
    return offs[:16].T.reshape(-1).astype(np.int64)


K, T, E, C, N = 512, 1024, 16, 128, 128


def by_expert(wq, xq):
    return np.concatenate([wq[e].T @ xq[:, e * C:(e + 1) * C] for e in range(E)], axis=1)


def setup_inputs():
    n = np.random.standard_normal
    s = mx_kscale(K)[:, None]
    first = np.random.permutation(np.repeat(np.arange(E), T // E))
    second = (first + 1 + np.random.permutation(np.repeat(np.arange(E - 1), -(-T // (E - 1)))[:T])) % E
    while np.bincount(second, minlength=E).max() != T // E:
        load = np.bincount(second, minlength=E); hi, lo = int(load.argmax()), int(load.argmin())
        t = np.flatnonzero((second == hi) & (first != lo))[0]; second[t] = lo
    slot_token = np.empty(E * C, np.int64); pos = np.empty((2, T), np.int64); fill = np.zeros(E, np.int64)
    place = np.stack([np.random.permutation(C) for _ in range(E)])
    for r, deal in enumerate((first, second)):
        for t in np.random.permutation(T):
            e = deal[t]; j = e * C + place[e, fill[e]]; fill[e] += 1; slot_token[j] = t; pos[r, t] = j
    g = np.random.uniform(0.2, 0.8, T)
    return {
        "xT": (n((K, T)) * s).astype(np.float32),
        "w": (n((E, K, N)) / np.sqrt(K) / s[None]).astype(np.float32),
        "gate": np.stack([np.tile(g, (N, 1)), np.tile(1.0 - g, (N, 1))]).astype(np.float32),
        "offs": striped(slot_token),
        "pos1": striped(pos[0]),
        "pos2": striped(pos[1]),
    }


def reference(xT, w, gate, offs, pos1, pos2):
    idx = unstriped(offs)
    xq = mxq(f64(xT)[:, idx], 0, "e4m3")
    y = by_expert(mxq(f64(w), 1, "e4m3"), xq)
    return f64(gate[0]) * y[:, unstriped(pos1)] + f64(gate[1]) * y[:, unstriped(pos2)]

@@ -1,0 +1,169 @@
+from contextlib import ExitStack
+
+import concourse.mybir as mybir
+
+K, T, E, C, N = 512, 1024, 16, 128, 128
+FLOPS = 2 * K * N * E * C
+
+F32 = mybir.dt.float32
+BF16 = mybir.dt.bfloat16
+U32 = mybir.dt.uint32
+U16 = mybir.dt.uint16
+U8 = mybir.dt.uint8
+FP8X4 = mybir.dt.float8_e4m3fn_x4
+MULT = mybir.AluOpType.mult
+ADD = mybir.AluOpType.add
+
+P = 128
+PACK = 4
+SLOTS = E * C
+CHUNKS = ((0, 512, "s"), (512, 512, "s"), (1024, 512, "s"), (1536, 256, "s"), (1792, 256, "v"))
+WGROUP = 4
+HALF = 512
+
+
+def tile_routed_moe_kernel(tc, xT, w, gate, offs, pos1, pos2, out):
+    nc = tc.nc
+    with ExitStack() as ctx:
+        lists = ctx.enter_context(tc.tile_pool(name="lists", bufs=1))
+        keep = ctx.enter_context(tc.tile_pool(name="keep", bufs=1))
+        psum = ctx.enter_context(tc.psum_pool(name="psum", bufs=1))
+
+        offs_sb = lists.tile([P, SLOTS // 16], U16, name="offs_sb")
+        nc.sync.dma_start(offs_sb[:], offs)
+        x_view = xT.rearrange("(p t) n -> p t n", t=PACK)
+        planes = []
+        for t in range(PACK):
+            plane = keep.tile([P, T], F32, name="plane%d" % t)
+            nc.sync.dma_start(plane[:], x_view[:, t, :])
+            planes.append(plane)
+        w_view = w.rearrange("e (p j) n -> p e (j n)", j=PACK)
+        w_raw = []
+        for g in range(E // WGROUP):
+            raw = keep.tile([P, WGROUP, PACK * N], F32, name="w_raw%d" % g)
+            nc.sync.dma_start(raw[:], w_view[:, g * WGROUP : (g + 1) * WGROUP, :])
+            w_raw.append(raw)
+        pos1_sb = lists.tile([P, T // 16], U16, name="pos1_sb")
+        nc.sync.dma_start(pos1_sb[:], pos1)
+        pos2_sb = lists.tile([P, T // 16], U16, name="pos2_sb")
+        nc.sync.dma_start(pos2_sb[:], pos2)
+        gate_sb = []
+        for r in range(2):
+            gt = keep.tile([P, T], F32, name="gate%d" % r)
+            nc.sync.dma_start(gt[:], gate[r])
+            gate_sb.append(gt)
+
+        y = keep.tile([P, SLOTS], F32, name="y")
+        banks = [psum.tile([P, WGROUP * C], F32, name="bank%d" % g) for g in range(E // WGROUP)]
+
+        gathered = {}
+        x_grouped = {}
+        x_codes = {}
+        x_scales = {}
+        w_codes = {}
+        w_scales = {}
+        w_grouped = {}
+
+        def gather(i):
+            s0, n, eng = CHUNKS[i]
+            g4 = keep.tile([P, PACK, n], F32, name="g4_%d" % i)
+            for t in range(PACK):
+                nc.vector.tensor_copy(g4[:, t, :], planes[t][:].indirect(offs_sb[:, s0 // 16 : (s0 + n) // 16]))
+            gathered[i] = g4
+
+        def interleave_tokens(i):
+            s0, n, eng = CHUNKS[i]
+            grp = keep.tile([P, n, PACK], BF16, name="xg_%d" % i, align_bytes=64)
+            src = gathered[i][:].rearrange("p t n -> p n t")
+            if eng == "s":
+                nc.scalar.copy(grp[:], src)
+            else:
+                nc.vector.tensor_copy(grp[:], src)
+            x_grouped[i] = grp
+
+        def quantize_tokens(i):
+            s0, n, eng = CHUNKS[i]
+            codes = keep.tile([P, n], U32, name="xc_%d" % i, align_bytes=64)
+            scales = keep.tile([P, n], U8, name="xs_%d" % i, align_bytes=64)
+            nc.vector.quantize_mx(
+                out=codes[:].bitcast(FP8X4),
+                scales=scales[:],
+                in_=x_grouped[i][:].rearrange("p n t -> p (n t)"),
+            )
+            x_codes[i] = codes
+            x_scales[i] = scales
+
+        def interleave_weights(g):
+            grp = keep.tile([P, WGROUP, N, PACK], BF16, name="wg_%d" % g, align_bytes=64)
+            nc.scalar.copy(grp[:], w_raw[g][:].rearrange("p e (j n) -> p e n j", j=PACK))
+            w_grouped[g] = grp
+
+        def quantize_weights(g):
+            codes = keep.tile([P, WGROUP * N], U32, name="wc_%d" % g, align_bytes=64)
+            scales = keep.tile([P, WGROUP * N], U8, name="ws_%d" % g, align_bytes=64)
+            nc.vector.quantize_mx(
+                out=codes[:].bitcast(FP8X4),
+                scales=scales[:],
+                in_=w_grouped[g][:].rearrange("p e n j -> p (e n j)"),
+            )
+            w_codes[g] = codes
+            w_scales[g] = scales
+
+        def multiply(i):
+            s0, n, eng = CHUNKS[i]
+            for e in range(s0 // C, (s0 + n) // C):
+                g, m = divmod(e, WGROUP)
+                wc = slice(m * N, (m + 1) * N)
+                xc = slice(e * C - s0, (e + 1) * C - s0)
+                nc.tensor.matmul_mx(
+                    out=banks[g][:, m * C : (m + 1) * C],
+                    lhsT=w_codes[g][:, wc].bitcast(FP8X4),
+                    lhsT_scale=w_scales[g][:, wc],
+                    rhs=x_codes[i][:, xc].bitcast(FP8X4),
+                    rhs_scale=x_scales[i][:, xc],
+                    start=True,
+                    stop=True,
+                )
+            g = s0 // (WGROUP * C)
+            b0 = s0 - g * WGROUP * C
+            nc.scalar.copy(y[:, s0 : s0 + n], banks[g][:, b0 : b0 + n])
+
+        gather(0)
+        interleave_tokens(0)
+        gather(1)
+        interleave_tokens(1)
+        interleave_weights(0)
+        quantize_weights(0)
+        quantize_tokens(0)
+        multiply(0)
+        gather(2)
+        interleave_tokens(2)
+        interleave_weights(1)
+        quantize_weights(1)
+        quantize_tokens(1)
+        multiply(1)
+        gather(3)
+        interleave_tokens(3)
+        interleave_weights(2)
+        quantize_weights(2)
+        quantize_tokens(2)
+        multiply(2)
+        gather(4)
+        interleave_weights(3)
+        quantize_weights(3)
+        quantize_tokens(3)
+        multiply(3)
+        interleave_tokens(4)
+        quantize_tokens(4)
+        multiply(4)
+
+        for h in range(T // HALF):
+            cols = slice(h * HALF, (h + 1) * HALF)
+            lcols = slice(h * HALF // 16, (h + 1) * HALF // 16)
+            first = keep.tile([P, HALF], F32, name="first%d" % h)
+            nc.vector.tensor_tensor(first[:], y[:].indirect(pos1_sb[:, lcols]), gate_sb[0][:, cols], MULT)
+            second = keep.tile([P, HALF], F32, name="second%d" % h)
+            nc.vector.tensor_tensor(second[:], y[:].indirect(pos2_sb[:, lcols]), gate_sb[1][:, cols], MULT)
+            total = keep.tile([P, HALF], F32, name="total%d" % h)
+            nc.vector.tensor_tensor(total[:], first[:], second[:], ADD)
+            nc.sync.dma_start(out[:, cols], total[:])

@@ -17,9 +17,13 @@ ADD = mybir.AluOpType.add
 P = 128
 PACK = 4
 SLOTS = E * C
-CHUNKS = ((0, 512, "s"), (512, 512, "s"), (1024, 512, "s"), (1536, 256, "s"), (1792, 256, "v"))
+
+CHUNKS = ((0, 512, "s", "s"), (512, 512, "v", "s"), (1024, 512, "v", "s"), (1536, 256, "s", "s"), (1792, 256, "s", "v"))
 WGROUP = 4
+W_ENGINE = ("s", "s", "s", "s")
 HALF = 512
+G4_BUFS = 3
+FAST = False
 
 
 def tile_routed_moe_kernel(tc, xT, w, gate, offs, pos1, pos2, out):
@@ -27,21 +31,29 @@ def tile_routed_moe_kernel(tc, xT, w, gate, offs, pos1, pos2, out):
     with ExitStack() as ctx:
         lists = ctx.enter_context(tc.tile_pool(name="lists", bufs=1))
         keep = ctx.enter_context(tc.tile_pool(name="keep", bufs=1))
+        ring = ctx.enter_context(tc.tile_pool(name="ring", bufs=G4_BUFS))
         psum = ctx.enter_context(tc.psum_pool(name="psum", bufs=1))
+
+        def copy(eng, dst, src):
+            if eng == "s":
+                nc.scalar.copy(dst, src)
+            elif eng == "g":
+                nc.gpsimd.tensor_copy(dst, src)
+            else:
+                nc.vector.tensor_copy(dst, src)
 
         offs_sb = lists.tile([P, SLOTS // 16], U16, name="offs_sb")
         nc.sync.dma_start(offs_sb[:], offs)
         x_view = xT.rearrange("(p t) n -> p t n", t=PACK)
+        w_view = w.rearrange("e (p j) n -> p e (j n)", j=PACK)
         planes = []
+        w_raw = []
         for t in range(PACK):
             plane = keep.tile([P, T], F32, name="plane%d" % t)
             nc.sync.dma_start(plane[:], x_view[:, t, :])
             planes.append(plane)
-        w_view = w.rearrange("e (p j) n -> p e (j n)", j=PACK)
-        w_raw = []
-        for g in range(E // WGROUP):
-            raw = keep.tile([P, WGROUP, PACK * N], F32, name="w_raw%d" % g)
-            nc.sync.dma_start(raw[:], w_view[:, g * WGROUP : (g + 1) * WGROUP, :])
+            raw = keep.tile([P, WGROUP, PACK * N], F32, name="w_raw%d" % t)
+            nc.sync.dma_start(raw[:], w_view[:, t * WGROUP : (t + 1) * WGROUP, :])
             w_raw.append(raw)
         pos1_sb = lists.tile([P, T // 16], U16, name="pos1_sb")
         nc.sync.dma_start(pos1_sb[:], pos1)
@@ -55,62 +67,55 @@ def tile_routed_moe_kernel(tc, xT, w, gate, offs, pos1, pos2, out):
 
         y = keep.tile([P, SLOTS], F32, name="y")
         banks = [psum.tile([P, WGROUP * C], F32, name="bank%d" % g) for g in range(E // WGROUP)]
-
-        gathered = {}
-        x_grouped = {}
-        x_codes = {}
-        x_scales = {}
+        w_grouped = {}
         w_codes = {}
         w_scales = {}
-        w_grouped = {}
-
-        def gather(i):
-            s0, n, eng = CHUNKS[i]
-            g4 = keep.tile([P, PACK, n], F32, name="g4_%d" % i)
-            for t in range(PACK):
-                nc.vector.tensor_copy(g4[:, t, :], planes[t][:].indirect(offs_sb[:, s0 // 16 : (s0 + n) // 16]))
-            gathered[i] = g4
-
-        def interleave_tokens(i):
-            s0, n, eng = CHUNKS[i]
-            grp = keep.tile([P, n, PACK], BF16, name="xg_%d" % i, align_bytes=64)
-            src = gathered[i][:].rearrange("p t n -> p n t")
-            if eng == "s":
-                nc.scalar.copy(grp[:], src)
-            else:
-                nc.vector.tensor_copy(grp[:], src)
-            x_grouped[i] = grp
-
-        def quantize_tokens(i):
-            s0, n, eng = CHUNKS[i]
-            codes = keep.tile([P, n], U32, name="xc_%d" % i, align_bytes=64)
-            scales = keep.tile([P, n], U8, name="xs_%d" % i, align_bytes=64)
-            nc.vector.quantize_mx(
-                out=codes[:].bitcast(FP8X4),
-                scales=scales[:],
-                in_=x_grouped[i][:].rearrange("p n t -> p (n t)"),
-            )
-            x_codes[i] = codes
-            x_scales[i] = scales
+        x_grouped = {}
 
         def interleave_weights(g):
             grp = keep.tile([P, WGROUP, N, PACK], BF16, name="wg_%d" % g, align_bytes=64)
-            nc.scalar.copy(grp[:], w_raw[g][:].rearrange("p e (j n) -> p e n j", j=PACK))
+            if FAST or W_ENGINE[g] == "g":
+                for m in range(WGROUP):
+                    if FAST:
+                        copy(
+                            W_ENGINE[g],
+                            grp[:, m, :, :].rearrange("p (c i) j -> p c j i", i=4),
+                            w_raw[g][:, m, :].rearrange("p (j c i) -> p c j i", j=PACK, i=4),
+                        )
+                    else:
+                        copy(W_ENGINE[g], grp[:, m, :, :], w_raw[g][:, m, :].rearrange("p (j n) -> p n j", j=PACK))
+            else:
+                copy(W_ENGINE[g], grp[:], w_raw[g][:].rearrange("p e (j n) -> p e n j", j=PACK))
             w_grouped[g] = grp
 
         def quantize_weights(g):
             codes = keep.tile([P, WGROUP * N], U32, name="wc_%d" % g, align_bytes=64)
             scales = keep.tile([P, WGROUP * N], U8, name="ws_%d" % g, align_bytes=64)
             nc.vector.quantize_mx(
-                out=codes[:].bitcast(FP8X4),
-                scales=scales[:],
-                in_=w_grouped[g][:].rearrange("p e n j -> p (e n j)"),
+                out=codes[:].bitcast(FP8X4), scales=scales[:], in_=w_grouped[g][:].rearrange("p e n j -> p (e n j)")
             )
             w_codes[g] = codes
             w_scales[g] = scales
 
+        def gather(i):
+            s0, n, eng, cpe = CHUNKS[i]
+            g4 = ring.tile([P, PACK, n], F32, name="g4_%d" % i, tag="g4")
+            for t in range(PACK):
+                nc.vector.tensor_copy(g4[:, t, :], planes[t][:].indirect(offs_sb[:, s0 // 16 : (s0 + n) // 16]))
+            grp = keep.tile([P, n, PACK], BF16, name="xg_%d" % i, align_bytes=64)
+            if FAST:
+                copy(eng, grp[:].rearrange("p (c i) t -> p c t i", i=4), g4[:].rearrange("p t (c i) -> p c t i", i=4))
+            else:
+                copy(eng, grp[:], g4[:].rearrange("p t n -> p n t"))
+            x_grouped[i] = grp
+
         def multiply(i):
-            s0, n, eng = CHUNKS[i]
+            s0, n, eng, cpe = CHUNKS[i]
+            codes = keep.tile([P, n], U32, name="xc_%d" % i, align_bytes=64)
+            scales = keep.tile([P, n], U8, name="xs_%d" % i, align_bytes=64)
+            nc.vector.quantize_mx(
+                out=codes[:].bitcast(FP8X4), scales=scales[:], in_=x_grouped[i][:].rearrange("p n t -> p (n t)")
+            )
             for e in range(s0 // C, (s0 + n) // C):
                 g, m = divmod(e, WGROUP)
                 wc = slice(m * N, (m + 1) * N)
@@ -119,43 +124,26 @@ def tile_routed_moe_kernel(tc, xT, w, gate, offs, pos1, pos2, out):
                     out=banks[g][:, m * C : (m + 1) * C],
                     lhsT=w_codes[g][:, wc].bitcast(FP8X4),
                     lhsT_scale=w_scales[g][:, wc],
-                    rhs=x_codes[i][:, xc].bitcast(FP8X4),
-                    rhs_scale=x_scales[i][:, xc],
+                    rhs=codes[:, xc].bitcast(FP8X4),
+                    rhs_scale=scales[:, xc],
                     start=True,
                     stop=True,
                 )
             g = s0 // (WGROUP * C)
             b0 = s0 - g * WGROUP * C
-            nc.scalar.copy(y[:, s0 : s0 + n], banks[g][:, b0 : b0 + n])
+            copy(cpe, y[:, s0 : s0 + n], banks[g][:, b0 : b0 + n])
 
-        gather(0)
-        interleave_tokens(0)
-        gather(1)
-        interleave_tokens(1)
-        interleave_weights(0)
-        quantize_weights(0)
-        quantize_tokens(0)
-        multiply(0)
-        gather(2)
-        interleave_tokens(2)
-        interleave_weights(1)
-        quantize_weights(1)
-        quantize_tokens(1)
-        multiply(1)
+        for g in range(E // WGROUP):
+            interleave_weights(g)
+        for i in range(3):
+            gather(i)
+        for g in range(E // WGROUP):
+            quantize_weights(g)
         gather(3)
-        interleave_tokens(3)
-        interleave_weights(2)
-        quantize_weights(2)
-        quantize_tokens(2)
-        multiply(2)
+        multiply(0)
         gather(4)
-        interleave_weights(3)
-        quantize_weights(3)
-        quantize_tokens(3)
-        multiply(3)
-        interleave_tokens(4)
-        quantize_tokens(4)
-        multiply(4)
+        for i in range(1, 5):
+            multiply(i)
 
         for h in range(T // HALF):
             cols = slice(h * HALF, (h + 1) * HALF)

@@ -23,7 +23,7 @@ WGROUP = 4
 W_ENGINE = ("s", "s", "s", "s")
 HALF = 512
 G4_BUFS = 3
-FAST = False
+FAST = True
 
 
 def tile_routed_moe_kernel(tc, xT, w, gate, offs, pos1, pos2, out):

@@ -18,11 +18,12 @@ P = 128
 PACK = 4
 SLOTS = E * C
 
-CHUNKS = ((0, 512, "s", "s"), (512, 512, "v", "s"), (1024, 512, "v", "s"), (1536, 256, "s", "s"), (1792, 256, "s", "v"))
+CHUNKS = ((0, 512, "s", "s"), (512, 512, "s", "s"), (1024, 512, "s", "s"), (1536, 256, "s", "v"), (1792, 256, "v", "v"))
 WGROUP = 4
 W_ENGINE = ("s", "s", "s", "s")
 HALF = 512
 G4_BUFS = 3
+LOADS = (("x", 0), ("w", 0), ("x", 1), ("w", 1), ("x", 2), ("w", 2), ("w", 3), ("x", 3))
 FAST = True
 
 
@@ -48,13 +49,15 @@ def tile_routed_moe_kernel(tc, xT, w, gate, offs, pos1, pos2, out):
         w_view = w.rearrange("e (p j) n -> p e (j n)", j=PACK)
         planes = []
         w_raw = []
-        for t in range(PACK):
-            plane = keep.tile([P, T], F32, name="plane%d" % t)
-            nc.sync.dma_start(plane[:], x_view[:, t, :])
-            planes.append(plane)
-            raw = keep.tile([P, WGROUP, PACK * N], F32, name="w_raw%d" % t)
-            nc.sync.dma_start(raw[:], w_view[:, t * WGROUP : (t + 1) * WGROUP, :])
-            w_raw.append(raw)
+        for kind, t in LOADS:
+            if kind == "x":
+                plane = keep.tile([P, T], F32, name="plane%d" % t)
+                nc.sync.dma_start(plane[:], x_view[:, t, :])
+                planes.append(plane)
+            else:
+                raw = keep.tile([P, WGROUP, PACK * N], F32, name="w_raw%d" % t)
+                nc.sync.dma_start(raw[:], w_view[:, t * WGROUP : (t + 1) * WGROUP, :])
+                w_raw.append(raw)
         pos1_sb = lists.tile([P, T // 16], U16, name="pos1_sb")
         nc.sync.dma_start(pos1_sb[:], pos1)
         pos2_sb = lists.tile([P, T // 16], U16, name="pos2_sb")
@@ -74,7 +77,13 @@ def tile_routed_moe_kernel(tc, xT, w, gate, offs, pos1, pos2, out):
 
         def interleave_weights(g):
             grp = keep.tile([P, WGROUP, N, PACK], BF16, name="wg_%d" % g, align_bytes=64)
-            if FAST or W_ENGINE[g] == "g":
+            if FAST and W_ENGINE[g] != "g":
+                copy(
+                    W_ENGINE[g],
+                    grp[:].rearrange("p e (c i) j -> p e c j i", i=4),
+                    w_raw[g][:].rearrange("p e (j c i) -> p e c j i", j=PACK, i=4),
+                )
+            elif FAST or W_ENGINE[g] == "g":
                 for m in range(WGROUP):
                     if FAST:
                         copy(

@@ -13,18 +13,23 @@ U8 = mybir.dt.uint8
 FP8X4 = mybir.dt.float8_e4m3fn_x4
 MULT = mybir.AluOpType.mult
 ADD = mybir.AluOpType.add
+COPY = mybir.ActivationFunctionType.Copy
 
 P = 128
 PACK = 4
 SLOTS = E * C
-
-CHUNKS = ((0, 512, "s", "s"), (512, 512, "s", "s"), (1024, 512, "s", "s"), (1536, 256, "s", "v"), (1792, 256, "v", "v"))
 WGROUP = 4
-W_ENGINE = ("s", "s", "s", "s")
 HALF = 512
-G4_BUFS = 3
-LOADS = (("x", 0), ("w", 0), ("x", 1), ("w", 1), ("x", 2), ("w", 2), ("w", 3), ("x", 3))
-FAST = True
+
+LOADS = (("x", 0), ("x", 1), ("x", 2), ("x", 3), ("w", 0), ("w", 1), ("w", 2), ("w", 3))
+CHUNKS = (
+    (0, 4, "v", "xc0", ((0, 4, "v"),)),
+    (4, 4, "s", "raw1", ((0, 4, "v"),)),
+    (8, 4, "s", "wg1", ((0, 4, "v"),)),
+    (12, 4, "s", "raw3", ((0, 2, "v"), (2, 1, "s"), (3, 1, "v"))),
+)
+S_PHASES = ((1, 2), (3,))
+XG_BUFS = 2
 
 
 def tile_routed_moe_kernel(tc, xT, w, gate, offs, pos1, pos2, out):
@@ -32,16 +37,8 @@ def tile_routed_moe_kernel(tc, xT, w, gate, offs, pos1, pos2, out):
     with ExitStack() as ctx:
         lists = ctx.enter_context(tc.tile_pool(name="lists", bufs=1))
         keep = ctx.enter_context(tc.tile_pool(name="keep", bufs=1))
-        ring = ctx.enter_context(tc.tile_pool(name="ring", bufs=G4_BUFS))
+        ring = ctx.enter_context(tc.tile_pool(name="ring", bufs=XG_BUFS))
         psum = ctx.enter_context(tc.psum_pool(name="psum", bufs=1))
-
-        def copy(eng, dst, src):
-            if eng == "s":
-                nc.scalar.copy(dst, src)
-            elif eng == "g":
-                nc.gpsimd.tensor_copy(dst, src)
-            else:
-                nc.vector.tensor_copy(dst, src)
 
         offs_sb = lists.tile([P, SLOTS // 16], U16, name="offs_sb")
         nc.sync.dma_start(offs_sb[:], offs)
@@ -55,7 +52,7 @@ def tile_routed_moe_kernel(tc, xT, w, gate, offs, pos1, pos2, out):
                 nc.sync.dma_start(plane[:], x_view[:, t, :])
                 planes.append(plane)
             else:
-                raw = keep.tile([P, WGROUP, PACK * N], F32, name="w_raw%d" % t)
+                raw = keep.tile([P, WGROUP, PACK * N], F32, name="w_raw%d" % t, tag="raw%d" % t, align_bytes=64)
                 nc.sync.dma_start(raw[:], w_view[:, t * WGROUP : (t + 1) * WGROUP, :])
                 w_raw.append(raw)
         pos1_sb = lists.tile([P, T // 16], U16, name="pos1_sb")
@@ -69,90 +66,86 @@ def tile_routed_moe_kernel(tc, xT, w, gate, offs, pos1, pos2, out):
             gate_sb.append(gt)
 
         y = keep.tile([P, SLOTS], F32, name="y")
-        banks = [psum.tile([P, WGROUP * C], F32, name="bank%d" % g) for g in range(E // WGROUP)]
-        w_grouped = {}
-        w_codes = {}
-        w_scales = {}
         x_grouped = {}
+        g4 = {}
+        for i, (e0, n, who, tag, pieces) in enumerate(CHUNKS):
+            if who == "v":
+                g4[i] = keep.tile([P, PACK, n * C], F32, name="g4_%d" % i)
+                x_grouped[i] = keep.tile([P, n * C, PACK], BF16, name="xgv_%d" % i, align_bytes=64)
 
-        def interleave_weights(g):
-            grp = keep.tile([P, WGROUP, N, PACK], BF16, name="wg_%d" % g, align_bytes=64)
-            if FAST and W_ENGINE[g] != "g":
-                copy(
-                    W_ENGINE[g],
-                    grp[:].rearrange("p e (c i) j -> p e c j i", i=4),
-                    w_raw[g][:].rearrange("p e (j c i) -> p e c j i", j=PACK, i=4),
-                )
-            elif FAST or W_ENGINE[g] == "g":
-                for m in range(WGROUP):
-                    if FAST:
-                        copy(
-                            W_ENGINE[g],
-                            grp[:, m, :, :].rearrange("p (c i) j -> p c j i", i=4),
-                            w_raw[g][:, m, :].rearrange("p (j c i) -> p c j i", j=PACK, i=4),
+        planes_bf = []
+        for t in range(PACK):
+            pb = keep.tile([P, T], BF16, name="plane_bf%d" % t)
+            nc.vector.tensor_copy(pb[:], planes[t][:])
+            planes_bf.append(pb)
+            for i, (e0, n, who, tag, pieces) in enumerate(CHUNKS):
+                if who == "v":
+                    nc.vector.tensor_copy(
+                        g4[i][:, t, :], planes[t][:].indirect(offs_sb[:, e0 * C // 16 : (e0 + n) * C // 16])
+                    )
+
+        for phase in S_PHASES:
+            for i in phase:
+                x_grouped[i] = ring.tile([P, CHUNKS[i][1] * C, PACK], BF16, name="xgs_%d" % i, tag="xgs", align_bytes=64)
+            for t in range(PACK):
+                for i in phase:
+                    e0, n = CHUNKS[i][0], CHUNKS[i][1]
+                    for m in range(n):
+                        e = e0 + m
+                        nc.scalar.activation(
+                            x_grouped[i][:, m * C : (m + 1) * C, t],
+                            planes_bf[t][:].indirect(offs_sb[:, e * C // 16 : (e + 1) * C // 16]),
+                            COPY,
                         )
-                    else:
-                        copy(W_ENGINE[g], grp[:, m, :, :], w_raw[g][:, m, :].rearrange("p (j n) -> p n j", j=PACK))
-            else:
-                copy(W_ENGINE[g], grp[:], w_raw[g][:].rearrange("p e (j n) -> p e n j", j=PACK))
-            w_grouped[g] = grp
 
-        def quantize_weights(g):
+        for i, (e0, n, who, tag, pieces) in enumerate(CHUNKS):
+            if who == "v":
+                nc.vector.tensor_copy(
+                    x_grouped[i][:].rearrange("p (c i) t -> p c t i", i=4), g4[i][:].rearrange("p t (c i) -> p c t i", i=4)
+                )
+
+        w_codes = []
+        w_scales = []
+        for g in range(E // WGROUP):
+            grp = keep.tile([P, WGROUP, N, PACK], BF16, name="wg_%d" % g, tag="wg%d" % g, align_bytes=64)
+            nc.vector.tensor_copy(
+                grp[:].rearrange("p e (c i) j -> p e c j i", i=4),
+                w_raw[g][:].rearrange("p e (j c i) -> p e c j i", j=PACK, i=4),
+            )
             codes = keep.tile([P, WGROUP * N], U32, name="wc_%d" % g, align_bytes=64)
             scales = keep.tile([P, WGROUP * N], U8, name="ws_%d" % g, align_bytes=64)
-            nc.vector.quantize_mx(
-                out=codes[:].bitcast(FP8X4), scales=scales[:], in_=w_grouped[g][:].rearrange("p e n j -> p (e n j)")
-            )
-            w_codes[g] = codes
-            w_scales[g] = scales
+            nc.vector.quantize_mx(out=codes[:].bitcast(FP8X4), scales=scales[:], in_=grp[:].rearrange("p e n j -> p (e n j)"))
+            w_codes.append(codes)
+            w_scales.append(scales)
 
-        def gather(i):
-            s0, n, eng, cpe = CHUNKS[i]
-            g4 = ring.tile([P, PACK, n], F32, name="g4_%d" % i, tag="g4")
-            for t in range(PACK):
-                nc.vector.tensor_copy(g4[:, t, :], planes[t][:].indirect(offs_sb[:, s0 // 16 : (s0 + n) // 16]))
-            grp = keep.tile([P, n, PACK], BF16, name="xg_%d" % i, align_bytes=64)
-            if FAST:
-                copy(eng, grp[:].rearrange("p (c i) t -> p c t i", i=4), g4[:].rearrange("p t (c i) -> p c t i", i=4))
-            else:
-                copy(eng, grp[:], g4[:].rearrange("p t n -> p n t"))
-            x_grouped[i] = grp
-
-        def multiply(i):
-            s0, n, eng, cpe = CHUNKS[i]
-            codes = keep.tile([P, n], U32, name="xc_%d" % i, align_bytes=64)
-            scales = keep.tile([P, n], U8, name="xs_%d" % i, align_bytes=64)
-            nc.vector.quantize_mx(
-                out=codes[:].bitcast(FP8X4), scales=scales[:], in_=x_grouped[i][:].rearrange("p n t -> p (n t)")
-            )
-            for e in range(s0 // C, (s0 + n) // C):
-                g, m = divmod(e, WGROUP)
-                wc = slice(m * N, (m + 1) * N)
-                xc = slice(e * C - s0, (e + 1) * C - s0)
-                nc.tensor.matmul_mx(
-                    out=banks[g][:, m * C : (m + 1) * C],
-                    lhsT=w_codes[g][:, wc].bitcast(FP8X4),
-                    lhsT_scale=w_scales[g][:, wc],
-                    rhs=codes[:, xc].bitcast(FP8X4),
-                    rhs_scale=scales[:, xc],
-                    start=True,
-                    stop=True,
+        for i, (e0, n, who, tag, pieces) in enumerate(CHUNKS):
+            codes = keep.tile([P, n * C], U32, name="xc_%d" % i, tag=tag, align_bytes=64)
+            scales = keep.tile([P, n * C], U8, name="xs_%d" % i, align_bytes=64)
+            flat = x_grouped[i][:].rearrange("p n t -> p (n t)")
+            for m0, k, cp in pieces:
+                cols = slice(m0 * C, (m0 + k) * C)
+                nc.vector.quantize_mx(
+                    out=codes[:, cols].bitcast(FP8X4), scales=scales[:, cols], in_=flat[:, m0 * C * PACK : (m0 + k) * C * PACK]
                 )
-            g = s0 // (WGROUP * C)
-            b0 = s0 - g * WGROUP * C
-            copy(cpe, y[:, s0 : s0 + n], banks[g][:, b0 : b0 + n])
-
-        for g in range(E // WGROUP):
-            interleave_weights(g)
-        for i in range(3):
-            gather(i)
-        for g in range(E // WGROUP):
-            quantize_weights(g)
-        gather(3)
-        multiply(0)
-        gather(4)
-        for i in range(1, 5):
-            multiply(i)
+                bank = psum.tile([P, k * C], F32, name="bank%d_%d" % (i, m0))
+                for m in range(m0, m0 + k):
+                    g, q = divmod(e0 + m, WGROUP)
+                    wc = slice(q * N, (q + 1) * N)
+                    xc = slice(m * C, (m + 1) * C)
+                    nc.tensor.matmul_mx(
+                        out=bank[:, (m - m0) * C : (m - m0 + 1) * C],
+                        lhsT=w_codes[g][:, wc].bitcast(FP8X4),
+                        lhsT_scale=w_scales[g][:, wc],
+                        rhs=codes[:, xc].bitcast(FP8X4),
+                        rhs_scale=scales[:, xc],
+                        start=True,
+                        stop=True,
+                    )
+                dst = y[:, (e0 + m0) * C : (e0 + m0 + k) * C]
+                if cp == "s":
+                    nc.scalar.copy(dst, bank[:])
+                else:
+                    nc.vector.tensor_copy(dst, bank[:])
 
         for h in range(T // HALF):
             cols = slice(h * HALF, (h + 1) * HALF)

@@ -19,17 +19,15 @@ P = 128
 PACK = 4
 SLOTS = E * C
 WGROUP = 4
-HALF = 512
+STORES = ((0, 768), (768, 1024))
 
-LOADS = (("x", 0), ("x", 1), ("x", 2), ("x", 3), ("w", 0), ("w", 1), ("w", 2), ("w", 3))
+LOADS = (("x", 0), ("x", 1), ("w", 0), ("x", 2), ("w", 1), ("x", 3), ("w", 2), ("w", 3))
 CHUNKS = (
-    (0, 4, "v", "xc0", ((0, 4, "v"),)),
-    (4, 4, "s", "raw1", ((0, 4, "v"),)),
-    (8, 4, "s", "wg1", ((0, 4, "v"),)),
-    (12, 4, "s", "raw3", ((0, 2, "v"), (2, 1, "s"), (3, 1, "v"))),
+    (0, 5, "v", "xg0", "xc0", ((0, 4, "v"), (4, 1, "v"))),
+    (5, 4, "s", "xg1", "raw1", ((0, 4, "s"),)),
+    (9, 4, "s", "xg2", "wg1", ((0, 4, "s"),)),
+    (13, 3, "s", "g4", "raw3", ((0, 1, "v"), (1, 1, "v"), (2, 1, "v"))),
 )
-S_PHASES = ((1, 2), (3,))
-XG_BUFS = 2
 
 
 def tile_routed_moe_kernel(tc, xT, w, gate, offs, pos1, pos2, out):
@@ -37,24 +35,21 @@ def tile_routed_moe_kernel(tc, xT, w, gate, offs, pos1, pos2, out):
     with ExitStack() as ctx:
         lists = ctx.enter_context(tc.tile_pool(name="lists", bufs=1))
         keep = ctx.enter_context(tc.tile_pool(name="keep", bufs=1))
-        ring = ctx.enter_context(tc.tile_pool(name="ring", bufs=XG_BUFS))
         psum = ctx.enter_context(tc.psum_pool(name="psum", bufs=1))
 
         offs_sb = lists.tile([P, SLOTS // 16], U16, name="offs_sb")
         nc.sync.dma_start(offs_sb[:], offs)
         x_view = xT.rearrange("(p t) n -> p t n", t=PACK)
         w_view = w.rearrange("e (p j) n -> p e (j n)", j=PACK)
-        planes = []
-        w_raw = []
+        planes = {}
+        w_raw = {}
         for kind, t in LOADS:
             if kind == "x":
-                plane = keep.tile([P, T], F32, name="plane%d" % t)
-                nc.sync.dma_start(plane[:], x_view[:, t, :])
-                planes.append(plane)
+                planes[t] = keep.tile([P, T], F32, name="plane%d" % t)
+                nc.sync.dma_start(planes[t][:], x_view[:, t, :])
             else:
-                raw = keep.tile([P, WGROUP, PACK * N], F32, name="w_raw%d" % t, tag="raw%d" % t, align_bytes=64)
-                nc.sync.dma_start(raw[:], w_view[:, t * WGROUP : (t + 1) * WGROUP, :])
-                w_raw.append(raw)
+                w_raw[t] = keep.tile([P, WGROUP, PACK * N], F32, name="w_raw%d" % t, tag="raw%d" % t, align_bytes=64)
+                nc.sync.dma_start(w_raw[t][:], w_view[:, t * WGROUP : (t + 1) * WGROUP, :])
         pos1_sb = lists.tile([P, T // 16], U16, name="pos1_sb")
         nc.sync.dma_start(pos1_sb[:], pos1)
         pos2_sb = lists.tile([P, T // 16], U16, name="pos2_sb")
@@ -66,29 +61,33 @@ def tile_routed_moe_kernel(tc, xT, w, gate, offs, pos1, pos2, out):
             gate_sb.append(gt)
 
         y = keep.tile([P, SLOTS], F32, name="y")
+        planes_bf = {}
         x_grouped = {}
-        g4 = {}
-        for i, (e0, n, who, tag, pieces) in enumerate(CHUNKS):
-            if who == "v":
-                g4[i] = keep.tile([P, PACK, n * C], F32, name="g4_%d" % i)
-                x_grouped[i] = keep.tile([P, n * C, PACK], BF16, name="xgv_%d" % i, align_bytes=64)
+        w_grouped = {}
+        w_codes = {}
+        w_scales = {}
+        g4 = keep.tile([P, PACK, CHUNKS[0][1] * C], F32, name="g4", tag="g4", align_bytes=64)
 
-        planes_bf = []
-        for t in range(PACK):
-            pb = keep.tile([P, T], BF16, name="plane_bf%d" % t)
-            nc.vector.tensor_copy(pb[:], planes[t][:])
-            planes_bf.append(pb)
-            for i, (e0, n, who, tag, pieces) in enumerate(CHUNKS):
-                if who == "v":
-                    nc.vector.tensor_copy(
-                        g4[i][:, t, :], planes[t][:].indirect(offs_sb[:, e0 * C // 16 : (e0 + n) * C // 16])
-                    )
+        def grouped_tile(i):
+            x_grouped[i] = keep.tile([P, CHUNKS[i][1] * C, PACK], BF16, name="xg_%d" % i, tag=CHUNKS[i][3], align_bytes=64)
 
-        for phase in S_PHASES:
-            for i in phase:
-                x_grouped[i] = ring.tile([P, CHUNKS[i][1] * C, PACK], BF16, name="xgs_%d" % i, tag="xgs", align_bytes=64)
+        def cast_and_gather(t):
+            planes_bf[t] = keep.tile([P, T], BF16, name="plane_bf%d" % t)
+            nc.vector.tensor_copy(planes_bf[t][:], planes[t][:])
+            e0, n = CHUNKS[0][0], CHUNKS[0][1]
+            nc.vector.tensor_copy(g4[:, t, :], planes[t][:].indirect(offs_sb[:, e0 * C // 16 : (e0 + n) * C // 16]))
+
+        def interleave_tokens():
+            grouped_tile(0)
+            nc.vector.tensor_copy(
+                x_grouped[0][:].rearrange("p (c i) t -> p c t i", i=4), g4[:].rearrange("p t (c i) -> p c t i", i=4)
+            )
+
+        def scalar_gathers(chunks):
+            for i in chunks:
+                grouped_tile(i)
             for t in range(PACK):
-                for i in phase:
+                for i in chunks:
                     e0, n = CHUNKS[i][0], CHUNKS[i][1]
                     for m in range(n):
                         e = e0 + m
@@ -98,28 +97,23 @@ def tile_routed_moe_kernel(tc, xT, w, gate, offs, pos1, pos2, out):
                             COPY,
                         )
 
-        for i, (e0, n, who, tag, pieces) in enumerate(CHUNKS):
-            if who == "v":
-                nc.vector.tensor_copy(
-                    x_grouped[i][:].rearrange("p (c i) t -> p c t i", i=4), g4[i][:].rearrange("p t (c i) -> p c t i", i=4)
-                )
-
-        w_codes = []
-        w_scales = []
-        for g in range(E // WGROUP):
-            grp = keep.tile([P, WGROUP, N, PACK], BF16, name="wg_%d" % g, tag="wg%d" % g, align_bytes=64)
+        def interleave_weights(g):
+            w_grouped[g] = keep.tile([P, WGROUP, N, PACK], BF16, name="wg_%d" % g, tag="wg%d" % g, align_bytes=64)
             nc.vector.tensor_copy(
-                grp[:].rearrange("p e (c i) j -> p e c j i", i=4),
+                w_grouped[g][:].rearrange("p e (c i) j -> p e c j i", i=4),
                 w_raw[g][:].rearrange("p e (j c i) -> p e c j i", j=PACK, i=4),
             )
-            codes = keep.tile([P, WGROUP * N], U32, name="wc_%d" % g, align_bytes=64)
-            scales = keep.tile([P, WGROUP * N], U8, name="ws_%d" % g, align_bytes=64)
-            nc.vector.quantize_mx(out=codes[:].bitcast(FP8X4), scales=scales[:], in_=grp[:].rearrange("p e n j -> p (e n j)"))
-            w_codes.append(codes)
-            w_scales.append(scales)
 
-        for i, (e0, n, who, tag, pieces) in enumerate(CHUNKS):
-            codes = keep.tile([P, n * C], U32, name="xc_%d" % i, tag=tag, align_bytes=64)
+        def quantize_weights(g):
+            w_codes[g] = keep.tile([P, WGROUP * N], U32, name="wc_%d" % g, align_bytes=64)
+            w_scales[g] = keep.tile([P, WGROUP * N], U8, name="ws_%d" % g, align_bytes=64)
+            nc.vector.quantize_mx(
+                out=w_codes[g][:].bitcast(FP8X4), scales=w_scales[g][:], in_=w_grouped[g][:].rearrange("p e n j -> p (e n j)")
+            )
+
+        def multiply(i):
+            e0, n, who, xtag, ctag, pieces = CHUNKS[i]
+            codes = keep.tile([P, n * C], U32, name="xc_%d" % i, tag=ctag, align_bytes=64)
             scales = keep.tile([P, n * C], U8, name="xs_%d" % i, align_bytes=64)
             flat = x_grouped[i][:].rearrange("p n t -> p (n t)")
             for m0, k, cp in pieces:
@@ -147,13 +141,29 @@ def tile_routed_moe_kernel(tc, xT, w, gate, offs, pos1, pos2, out):
                 else:
                     nc.vector.tensor_copy(dst, bank[:])
 
-        for h in range(T // HALF):
-            cols = slice(h * HALF, (h + 1) * HALF)
-            lcols = slice(h * HALF // 16, (h + 1) * HALF // 16)
-            first = keep.tile([P, HALF], F32, name="first%d" % h)
-            nc.vector.tensor_tensor(first[:], y[:].indirect(pos1_sb[:, lcols]), gate_sb[0][:, cols], MULT)
-            second = keep.tile([P, HALF], F32, name="second%d" % h)
-            nc.vector.tensor_tensor(second[:], y[:].indirect(pos2_sb[:, lcols]), gate_sb[1][:, cols], MULT)
-            total = keep.tile([P, HALF], F32, name="total%d" % h)
+        for t in range(PACK):
+            cast_and_gather(t)
+        scalar_gathers((1, 2))
+        interleave_weights(0)
+        quantize_weights(0)
+        interleave_weights(1)
+        quantize_weights(1)
+        interleave_tokens()
+        scalar_gathers((3,))
+        interleave_weights(2)
+        multiply(0)
+        quantize_weights(2)
+        multiply(1)
+        interleave_weights(3)
+        quantize_weights(3)
+        multiply(2)
+        multiply(3)
+
+        for h, (c0, c1) in enumerate(STORES):
+            first = keep.tile([P, c1 - c0], F32, name="first%d" % h)
+            nc.vector.tensor_tensor(first[:], y[:].indirect(pos1_sb[:, c0 // 16 : c1 // 16]), gate_sb[0][:, c0:c1], MULT)
+            second = keep.tile([P, c1 - c0], F32, name="second%d" % h)
+            nc.vector.tensor_tensor(second[:], y[:].indirect(pos2_sb[:, c0 // 16 : c1 // 16]), gate_sb[1][:, c0:c1], MULT)
+            total = keep.tile([P, c1 - c0], F32, name="total%d" % h)
             nc.vector.tensor_tensor(total[:], first[:], second[:], ADD)
-            nc.sync.dma_start(out[:, cols], total[:])
+            nc.sync.dma_start(out[:, c0:c1], total[:])

@@ -21,6 +21,7 @@ SLOTS = E * C
 WGROUP = 4
 STORES = ((0, 768), (768, 1024))
 
+PIECES = (4, 1, 1, 1)
 LOADS = (("x", 0), ("x", 1), ("w", 0), ("x", 2), ("w", 1), ("x", 3), ("w", 2), ("w", 3))
 CHUNKS = (
     (0, 5, "v", "xg0", "xc0", ((0, 4, "v"), (4, 1, "v"))),
@@ -37,8 +38,11 @@ def tile_routed_moe_kernel(tc, xT, w, gate, offs, pos1, pos2, out):
         keep = ctx.enter_context(tc.tile_pool(name="keep", bufs=1))
         psum = ctx.enter_context(tc.psum_pool(name="psum", bufs=1))
 
+        warm = keep.tile([P, 2], F32, name="warm")
+        nc.gpsimd.memset(warm[:, 0:1], 0.0)
+        nc.scalar.activation(warm[:, 1:2], warm[:, 0:1], COPY)
+
         offs_sb = lists.tile([P, SLOTS // 16], U16, name="offs_sb")
-        nc.sync.dma_start(offs_sb[:], offs)
         x_view = xT.rearrange("(p t) n -> p t n", t=PACK)
         w_view = w.rearrange("e (p j) n -> p e (j n)", j=PACK)
         planes = {}
@@ -46,7 +50,11 @@ def tile_routed_moe_kernel(tc, xT, w, gate, offs, pos1, pos2, out):
         for kind, t in LOADS:
             if kind == "x":
                 planes[t] = keep.tile([P, T], F32, name="plane%d" % t)
-                nc.sync.dma_start(planes[t][:], x_view[:, t, :])
+                step = T // PIECES[t]
+                for c0 in range(0, T, step):
+                    nc.sync.dma_start(planes[t][:, c0 : c0 + step], x_view[:, t, c0 : c0 + step])
+                if t == 0:
+                    nc.sync.dma_start(offs_sb[:], offs)
             else:
                 w_raw[t] = keep.tile([P, WGROUP, PACK * N], F32, name="w_raw%d" % t, tag="raw%d" % t, align_bytes=64)
                 nc.sync.dma_start(w_raw[t][:], w_view[:, t * WGROUP : (t + 1) * WGROUP, :])
@@ -73,7 +81,9 @@ def tile_routed_moe_kernel(tc, xT, w, gate, offs, pos1, pos2, out):
 
         def cast_and_gather(t):
             planes_bf[t] = keep.tile([P, T], BF16, name="plane_bf%d" % t)
-            nc.vector.tensor_copy(planes_bf[t][:], planes[t][:])
+            step = T // PIECES[t]
+            for c0 in range(0, T, step):
+                nc.vector.tensor_copy(planes_bf[t][:, c0 : c0 + step], planes[t][:, c0 : c0 + step])
             e0, n = CHUNKS[0][0], CHUNKS[0][1]
             nc.vector.tensor_copy(g4[:, t, :], planes[t][:].indirect(offs_sb[:, e0 * C // 16 : (e0 + n) * C // 16]))
 

@@ -22,12 +22,14 @@ WGROUP = 4
 STORES = ((0, 768), (768, 1024))
 
 PIECES = (4, 1, 1, 1)
-LOADS = (("x", 0), ("x", 1), ("w", 0), ("x", 2), ("w", 1), ("x", 3), ("w", 2), ("w", 3))
+LOADS = (("x", 0), ("x", 1), ("x", 2), ("x", 3), ("w", 0), ("w", 1), ("w", 2), ("w", 3))
+CASTERS = ("v", "g", "g", "g")
+G_GROUP = 0
 CHUNKS = (
-    (0, 5, "v", "xg0", "xc0", ((0, 4, "v"), (4, 1, "v"))),
-    (5, 4, "s", "xg1", "raw1", ((0, 4, "s"),)),
-    (9, 4, "s", "xg2", "wg1", ((0, 4, "s"),)),
-    (13, 3, "s", "g4", "raw3", ((0, 1, "v"), (1, 1, "v"), (2, 1, "v"))),
+    (0, 6, "v", "xg0", "raw1", ((0, 4, "s"), (4, 2, "s"))),
+    (6, 4, "s", "xg1", "wg1", ((0, 4, "s"),)),
+    (10, 4, "s", "xg2", "wg2", ((0, 4, "s"),)),
+    (14, 2, "s", "g4", "wg3", ((0, 1, "v"), (1, 1, "v"))),
 )
 
 
@@ -57,7 +59,9 @@ def tile_routed_moe_kernel(tc, xT, w, gate, offs, pos1, pos2, out):
                     nc.sync.dma_start(offs_sb[:], offs)
             else:
                 w_raw[t] = keep.tile([P, WGROUP, PACK * N], F32, name="w_raw%d" % t, tag="raw%d" % t, align_bytes=64)
-                nc.sync.dma_start(w_raw[t][:], w_view[:, t * WGROUP : (t + 1) * WGROUP, :])
+                step = 1 if t == G_GROUP else WGROUP
+                for q in range(0, WGROUP, step):
+                    nc.sync.dma_start(w_raw[t][:, q : q + step, :], w_view[:, t * WGROUP + q : t * WGROUP + q + step, :])
         pos1_sb = lists.tile([P, T // 16], U16, name="pos1_sb")
         nc.sync.dma_start(pos1_sb[:], pos1)
         pos2_sb = lists.tile([P, T // 16], U16, name="pos2_sb")
@@ -83,7 +87,8 @@ def tile_routed_moe_kernel(tc, xT, w, gate, offs, pos1, pos2, out):
             planes_bf[t] = keep.tile([P, T], BF16, name="plane_bf%d" % t)
             step = T // PIECES[t]
             for c0 in range(0, T, step):
-                nc.vector.tensor_copy(planes_bf[t][:, c0 : c0 + step], planes[t][:, c0 : c0 + step])
+                caster = nc.gpsimd if CASTERS[t] == "g" else nc.vector
+                caster.tensor_copy(planes_bf[t][:, c0 : c0 + step], planes[t][:, c0 : c0 + step])
             e0, n = CHUNKS[0][0], CHUNKS[0][1]
             nc.vector.tensor_copy(g4[:, t, :], planes[t][:].indirect(offs_sb[:, e0 * C // 16 : (e0 + n) * C // 16]))
 
@@ -109,13 +114,17 @@ def tile_routed_moe_kernel(tc, xT, w, gate, offs, pos1, pos2, out):
 
         def interleave_weights(g):
             w_grouped[g] = keep.tile([P, WGROUP, N, PACK], BF16, name="wg_%d" % g, tag="wg%d" % g, align_bytes=64)
+            if g == G_GROUP:
+                for q in range(WGROUP):
+                    nc.gpsimd.tensor_copy(w_grouped[g][:, q], w_raw[g][:, q].rearrange("p (j n) -> p n j", j=PACK))
+                return
             nc.vector.tensor_copy(
                 w_grouped[g][:].rearrange("p e (c i) j -> p e c j i", i=4),
                 w_raw[g][:].rearrange("p e (j c i) -> p e c j i", j=PACK, i=4),
             )
 
         def quantize_weights(g):
-            w_codes[g] = keep.tile([P, WGROUP * N], U32, name="wc_%d" % g, align_bytes=64)
+            w_codes[g] = keep.tile([P, WGROUP * N], U32, name="wc_%d" % g, tag=("wc0", "raw2", "raw3", "wc3")[g], align_bytes=64)
             w_scales[g] = keep.tile([P, WGROUP * N], U8, name="ws_%d" % g, align_bytes=64)
             nc.vector.quantize_mx(
                 out=w_codes[g][:].bitcast(FP8X4), scales=w_scales[g][:], in_=w_grouped[g][:].rearrange("p e n j -> p (e n j)")
@@ -155,16 +164,16 @@ def tile_routed_moe_kernel(tc, xT, w, gate, offs, pos1, pos2, out):
             cast_and_gather(t)
         scalar_gathers((1, 2))
         interleave_weights(0)
+        interleave_tokens()
         quantize_weights(0)
         interleave_weights(1)
-        quantize_weights(1)
-        interleave_tokens()
-        scalar_gathers((3,))
         interleave_weights(2)
+        quantize_weights(1)
+        scalar_gathers((3,))
         multiply(0)
+        interleave_weights(3)
         quantize_weights(2)
         multiply(1)
-        interleave_weights(3)
         quantize_weights(3)
         multiply(2)
         multiply(3)

@@ -1,6 +1,7 @@
 from contextlib import ExitStack
 
 import concourse.mybir as mybir
+from concourse.masks import make_identity
 
 K, T, E, C, N = 512, 1024, 16, 128, 128
 FLOPS = 2 * K * N * E * C
@@ -19,18 +20,32 @@ P = 128
 PACK = 4
 SLOTS = E * C
 WGROUP = 4
-STORES = ((0, 768), (768, 1024))
+
+STORES = ((0, 384, "t"), (384, 768, "v"), (768, 1024, "v"))
 
 PIECES = (4, 1, 1, 1)
-LOADS = (("x", 0), ("x", 1), ("x", 2), ("x", 3), ("w", 0), ("w", 1), ("w", 2), ("w", 3))
 CASTERS = ("v", "g", "g", "g")
-G_GROUP = 0
-CHUNKS = (
-    (0, 6, "v", "xg0", "raw1", ((0, 4, "s"), (4, 2, "s"))),
-    (6, 4, "s", "xg1", "wg1", ((0, 4, "s"),)),
-    (10, 4, "s", "xg2", "wg2", ((0, 4, "s"),)),
-    (14, 2, "s", "g4", "wg3", ((0, 1, "v"), (1, 1, "v"))),
+G_EXPERTS = 2
+LOADS = (
+    ("x", 0),
+    ("x", 1),
+    ("x", 2),
+    ("x", 3),
+    ("w", 0, 1),
+    ("w", 1, 1),
+    ("w", 2, 2),
+    ("w", 4, 4),
+    ("w", 8, 4),
+    ("w", 12, 4),
 )
+RAW_TAGS = {0: "raw_e0", 1: "raw_e1", 2: "raw_e2", 4: "raw1", 8: "raw2", 12: "raw3"}
+CHUNKS = (
+    (0, 5, "raw_e2", "raw1", ((0, 4, "s"), (4, 1, "s"))),
+    (5, 4, "xg1", "wg1", ((0, 4, "s"),)),
+    (9, 4, "xg2", "wg2", ((0, 4, "s"),)),
+    (13, 3, "g4", "xg2", ((0, 2, "v"), (2, 1, "v"))),
+)
+WC_TAGS = ("wc0", "raw2", "raw3", "wc3")
 
 
 def tile_routed_moe_kernel(tc, xT, w, gate, offs, pos1, pos2, out):
@@ -49,8 +64,9 @@ def tile_routed_moe_kernel(tc, xT, w, gate, offs, pos1, pos2, out):
         w_view = w.rearrange("e (p j) n -> p e (j n)", j=PACK)
         planes = {}
         w_raw = {}
-        for kind, t in LOADS:
-            if kind == "x":
+        for load in LOADS:
+            if load[0] == "x":
+                t = load[1]
                 planes[t] = keep.tile([P, T], F32, name="plane%d" % t)
                 step = T // PIECES[t]
                 for c0 in range(0, T, step):
@@ -58,10 +74,9 @@ def tile_routed_moe_kernel(tc, xT, w, gate, offs, pos1, pos2, out):
                 if t == 0:
                     nc.sync.dma_start(offs_sb[:], offs)
             else:
-                w_raw[t] = keep.tile([P, WGROUP, PACK * N], F32, name="w_raw%d" % t, tag="raw%d" % t, align_bytes=64)
-                step = 1 if t == G_GROUP else WGROUP
-                for q in range(0, WGROUP, step):
-                    nc.sync.dma_start(w_raw[t][:, q : q + step, :], w_view[:, t * WGROUP + q : t * WGROUP + q + step, :])
+                e, k = load[1], load[2]
+                w_raw[e] = keep.tile([P, k, PACK * N], F32, name="w_raw%d" % e, tag=RAW_TAGS[e], align_bytes=64)
+                nc.sync.dma_start(w_raw[e][:], w_view[:, e : e + k, :])
         pos1_sb = lists.tile([P, T // 16], U16, name="pos1_sb")
         nc.sync.dma_start(pos1_sb[:], pos1)
         pos2_sb = lists.tile([P, T // 16], U16, name="pos2_sb")
@@ -75,13 +90,16 @@ def tile_routed_moe_kernel(tc, xT, w, gate, offs, pos1, pos2, out):
         y = keep.tile([P, SLOTS], F32, name="y")
         planes_bf = {}
         x_grouped = {}
+        x_codes = {}
+        x_scales = {}
         w_grouped = {}
         w_codes = {}
         w_scales = {}
+        g2 = keep.tile([P, 2, C], F32, name="g2")
         g4 = keep.tile([P, PACK, CHUNKS[0][1] * C], F32, name="g4", tag="g4", align_bytes=64)
 
         def grouped_tile(i):
-            x_grouped[i] = keep.tile([P, CHUNKS[i][1] * C, PACK], BF16, name="xg_%d" % i, tag=CHUNKS[i][3], align_bytes=64)
+            x_grouped[i] = keep.tile([P, CHUNKS[i][1] * C, PACK], BF16, name="xg_%d" % i, tag=CHUNKS[i][2], align_bytes=64)
 
         def cast_and_gather(t):
             planes_bf[t] = keep.tile([P, T], BF16, name="plane_bf%d" % t)
@@ -92,54 +110,60 @@ def tile_routed_moe_kernel(tc, xT, w, gate, offs, pos1, pos2, out):
             e0, n = CHUNKS[0][0], CHUNKS[0][1]
             nc.vector.tensor_copy(g4[:, t, :], planes[t][:].indirect(offs_sb[:, e0 * C // 16 : (e0 + n) * C // 16]))
 
+            if t >= 2:
+                e = E - 1
+                nc.vector.tensor_copy(g2[:, t - 2, :], planes[t][:].indirect(offs_sb[:, e * C // 16 : (e + 1) * C // 16]))
+
         def interleave_tokens():
             grouped_tile(0)
             nc.vector.tensor_copy(
                 x_grouped[0][:].rearrange("p (c i) t -> p c t i", i=4), g4[:].rearrange("p t (c i) -> p c t i", i=4)
             )
 
-        def scalar_gathers(chunks):
-            for i in chunks:
-                grouped_tile(i)
-            for t in range(PACK):
-                for i in chunks:
-                    e0, n = CHUNKS[i][0], CHUNKS[i][1]
-                    for m in range(n):
-                        e = e0 + m
-                        nc.scalar.activation(
-                            x_grouped[i][:, m * C : (m + 1) * C, t],
-                            planes_bf[t][:].indirect(offs_sb[:, e * C // 16 : (e + 1) * C // 16]),
-                            COPY,
-                        )
-
-        def interleave_weights(g):
-            w_grouped[g] = keep.tile([P, WGROUP, N, PACK], BF16, name="wg_%d" % g, tag="wg%d" % g, align_bytes=64)
-            if g == G_GROUP:
-                for q in range(WGROUP):
-                    nc.gpsimd.tensor_copy(w_grouped[g][:, q], w_raw[g][:, q].rearrange("p (j n) -> p n j", j=PACK))
-                return
-            nc.vector.tensor_copy(
-                w_grouped[g][:].rearrange("p e (c i) j -> p e c j i", i=4),
-                w_raw[g][:].rearrange("p e (j c i) -> p e c j i", j=PACK, i=4),
+        def gather_expert(i, m, t):
+            e = CHUNKS[i][0] + m
+            nc.scalar.activation(
+                x_grouped[i][:, m * C : (m + 1) * C, t],
+                planes_bf[t][:].indirect(offs_sb[:, e * C // 16 : (e + 1) * C // 16]),
+                COPY,
             )
 
+        def interleave_weights(e):
+            g, q = divmod(e, WGROUP)
+            k = w_raw[e][:].shape[1]
+            if g not in w_grouped:
+                w_grouped[g] = keep.tile([P, WGROUP, N, PACK], BF16, name="wg_%d" % g, tag="wg%d" % g, align_bytes=64)
+            if e < G_EXPERTS:
+                nc.gpsimd.tensor_copy(w_grouped[g][:, q], w_raw[e][:, 0].rearrange("p (j n) -> p n j", j=PACK))
+            else:
+                nc.vector.tensor_copy(
+                    w_grouped[g][:, q : q + k].rearrange("p e (c i) j -> p e c j i", i=4),
+                    w_raw[e][:].rearrange("p e (j c i) -> p e c j i", j=PACK, i=4),
+                )
+
         def quantize_weights(g):
-            w_codes[g] = keep.tile([P, WGROUP * N], U32, name="wc_%d" % g, tag=("wc0", "raw2", "raw3", "wc3")[g], align_bytes=64)
+            w_codes[g] = keep.tile([P, WGROUP * N], U32, name="wc_%d" % g, tag=WC_TAGS[g], align_bytes=64)
             w_scales[g] = keep.tile([P, WGROUP * N], U8, name="ws_%d" % g, align_bytes=64)
             nc.vector.quantize_mx(
                 out=w_codes[g][:].bitcast(FP8X4), scales=w_scales[g][:], in_=w_grouped[g][:].rearrange("p e n j -> p (e n j)")
             )
 
-        def multiply(i):
-            e0, n, who, xtag, ctag, pieces = CHUNKS[i]
-            codes = keep.tile([P, n * C], U32, name="xc_%d" % i, tag=ctag, align_bytes=64)
-            scales = keep.tile([P, n * C], U8, name="xs_%d" % i, align_bytes=64)
+        def quantize_tokens(i):
+            n, pieces = CHUNKS[i][1], CHUNKS[i][4]
+            x_codes[i] = keep.tile([P, n * C], U32, name="xc_%d" % i, tag=CHUNKS[i][3], align_bytes=64)
+            x_scales[i] = keep.tile([P, n * C], U8, name="xs_%d" % i, align_bytes=64)
             flat = x_grouped[i][:].rearrange("p n t -> p (n t)")
             for m0, k, cp in pieces:
                 cols = slice(m0 * C, (m0 + k) * C)
                 nc.vector.quantize_mx(
-                    out=codes[:, cols].bitcast(FP8X4), scales=scales[:, cols], in_=flat[:, m0 * C * PACK : (m0 + k) * C * PACK]
+                    out=x_codes[i][:, cols].bitcast(FP8X4),
+                    scales=x_scales[i][:, cols],
+                    in_=flat[:, m0 * C * PACK : (m0 + k) * C * PACK],
                 )
+
+        def multiply(i):
+            e0, pieces = CHUNKS[i][0], CHUNKS[i][4]
+            for m0, k, cp in pieces:
                 bank = psum.tile([P, k * C], F32, name="bank%d_%d" % (i, m0))
                 for m in range(m0, m0 + k):
                     g, q = divmod(e0 + m, WGROUP)
@@ -149,8 +173,8 @@ def tile_routed_moe_kernel(tc, xT, w, gate, offs, pos1, pos2, out):
                         out=bank[:, (m - m0) * C : (m - m0 + 1) * C],
                         lhsT=w_codes[g][:, wc].bitcast(FP8X4),
                         lhsT_scale=w_scales[g][:, wc],
-                        rhs=codes[:, xc].bitcast(FP8X4),
-                        rhs_scale=scales[:, xc],
+                        rhs=x_codes[i][:, xc].bitcast(FP8X4),
+                        rhs_scale=x_scales[i][:, xc],
                         start=True,
                         stop=True,
                     )
@@ -162,27 +186,50 @@ def tile_routed_moe_kernel(tc, xT, w, gate, offs, pos1, pos2, out):
 
         for t in range(PACK):
             cast_and_gather(t)
-        scalar_gathers((1, 2))
         interleave_weights(0)
-        interleave_tokens()
-        quantize_weights(0)
+        for i in (1, 2):
+            grouped_tile(i)
+        for t in range(PACK):
+            for i in (1, 2):
+                for m in range(CHUNKS[i][1]):
+                    gather_expert(i, m, t)
         interleave_weights(1)
         interleave_weights(2)
+        interleave_tokens()
+        grouped_tile(3)
+        for m in range(CHUNKS[3][1]):
+            for t in range(PACK if m < 2 else 2):
+                gather_expert(3, m, t)
+        nc.vector.tensor_copy(x_grouped[3][:, 2 * C : 3 * C, 2:4], g2[:].rearrange("p t c -> p c t"))
+        quantize_weights(0)
+        interleave_weights(4)
+        quantize_tokens(0)
+        interleave_weights(8)
         quantize_weights(1)
-        scalar_gathers((3,))
         multiply(0)
-        interleave_weights(3)
+        quantize_tokens(1)
+        interleave_weights(12)
         quantize_weights(2)
         multiply(1)
+        quantize_tokens(2)
         quantize_weights(3)
         multiply(2)
+        quantize_tokens(3)
         multiply(3)
 
-        for h, (c0, c1) in enumerate(STORES):
+        identity = keep.tile([P, P], F32, name="identity")
+        make_identity(nc, identity[:])
+        for h, (c0, c1, adder) in enumerate(STORES):
             first = keep.tile([P, c1 - c0], F32, name="first%d" % h)
             nc.vector.tensor_tensor(first[:], y[:].indirect(pos1_sb[:, c0 // 16 : c1 // 16]), gate_sb[0][:, c0:c1], MULT)
             second = keep.tile([P, c1 - c0], F32, name="second%d" % h)
             nc.vector.tensor_tensor(second[:], y[:].indirect(pos2_sb[:, c0 // 16 : c1 // 16]), gate_sb[1][:, c0:c1], MULT)
             total = keep.tile([P, c1 - c0], F32, name="total%d" % h)
-            nc.vector.tensor_tensor(total[:], first[:], second[:], ADD)
+            if adder == "t":
+                acc = psum.tile([P, c1 - c0], F32, name="acc")
+                nc.tensor.matmul(acc[:], identity[:], first[:], start=True, stop=False)
+                nc.tensor.matmul(acc[:], identity[:], second[:], start=False, stop=True)
+                nc.scalar.copy(total[:], acc[:])
+            else:
+                nc.vector.tensor_tensor(total[:], first[:], second[:], ADD)
             nc.sync.dma_start(out[:, c0:c1], total[:])

@@ -1,7 +1,6 @@
 from contextlib import ExitStack
 
 import concourse.mybir as mybir
-from concourse.masks import make_identity
 
 K, T, E, C, N = 512, 1024, 16, 128, 128
 FLOPS = 2 * K * N * E * C
@@ -21,7 +20,7 @@ PACK = 4
 SLOTS = E * C
 WGROUP = 4
 
-STORES = ((0, 384, "t"), (384, 768, "v"), (768, 1024, "v"))
+STORES = ((0, 768), (768, 1024))
 
 PIECES = (4, 1, 1, 1)
 CASTERS = ("v", "g", "g", "g")
@@ -217,19 +216,11 @@ def tile_routed_moe_kernel(tc, xT, w, gate, offs, pos1, pos2, out):
         quantize_tokens(3)
         multiply(3)
 
-        identity = keep.tile([P, P], F32, name="identity")
-        make_identity(nc, identity[:])
-        for h, (c0, c1, adder) in enumerate(STORES):
+        for h, (c0, c1) in enumerate(STORES):
             first = keep.tile([P, c1 - c0], F32, name="first%d" % h)
             nc.vector.tensor_tensor(first[:], y[:].indirect(pos1_sb[:, c0 // 16 : c1 // 16]), gate_sb[0][:, c0:c1], MULT)
             second = keep.tile([P, c1 - c0], F32, name="second%d" % h)
             nc.vector.tensor_tensor(second[:], y[:].indirect(pos2_sb[:, c0 // 16 : c1 // 16]), gate_sb[1][:, c0:c1], MULT)
             total = keep.tile([P, c1 - c0], F32, name="total%d" % h)
-            if adder == "t":
-                acc = psum.tile([P, c1 - c0], F32, name="acc")
-                nc.tensor.matmul(acc[:], identity[:], first[:], start=True, stop=False)
-                nc.tensor.matmul(acc[:], identity[:], second[:], start=False, stop=True)
-                nc.scalar.copy(total[:], acc[:])
-            else:
-                nc.vector.tensor_tensor(total[:], first[:], second[:], ADD)
+            nc.vector.tensor_tensor(total[:], first[:], second[:], ADD)
             nc.sync.dma_start(out[:, c0:c1], total[:])

@@ -19,7 +19,6 @@ P = 128
 PACK = 4
 SLOTS = E * C
 WGROUP = 4
-
 STORES = ((0, 768), (768, 1024))
 
 PIECES = (4, 1, 1, 1)
@@ -38,13 +37,13 @@ LOADS = (
     ("w", 12, 4),
 )
 RAW_TAGS = {0: "raw_e0", 1: "raw_e1", 2: "raw_e2", 4: "raw1", 8: "raw2", 12: "raw3"}
-CHUNKS = (
-    (0, 5, "raw_e2", "raw1", ((0, 4, "s"), (4, 1, "s"))),
-    (5, 4, "xg1", "wg1", ((0, 4, "s"),)),
-    (9, 4, "xg2", "wg2", ((0, 4, "s"),)),
-    (13, 3, "g4", "xg2", ((0, 2, "v"), (2, 1, "v"))),
-)
 WC_TAGS = ("wc0", "raw2", "raw3", "wc3")
+V_EXPERTS = 5
+CHUNKS = (
+    ((0, 1, 2, 3, 4), "raw_e2", "raw1", ((0, 4), (4, 1)), ((0, 4, "s"), (4, 1, "s"))),
+    ((6, 7, 8, 9, 10, 11, 12, 13), "xg1", "wg1", ((0, 8),), ((0, 4, "s"), (4, 4, "s"))),
+    ((14, 15, 5), "raw_e1", "wg2", ((0, 2), (2, 1)), ((0, 2, "v"), (2, 1, "v"))),
+)
 
 
 def tile_routed_moe_kernel(tc, xT, w, gate, offs, pos1, pos2, out):
@@ -94,11 +93,10 @@ def tile_routed_moe_kernel(tc, xT, w, gate, offs, pos1, pos2, out):
         w_grouped = {}
         w_codes = {}
         w_scales = {}
-        g2 = keep.tile([P, 2, C], F32, name="g2")
-        g4 = keep.tile([P, PACK, CHUNKS[0][1] * C], F32, name="g4", tag="g4", align_bytes=64)
+        g4 = keep.tile([P, PACK, (V_EXPERTS + 1) * C], F32, name="g4")
 
         def grouped_tile(i):
-            x_grouped[i] = keep.tile([P, CHUNKS[i][1] * C, PACK], BF16, name="xg_%d" % i, tag=CHUNKS[i][2], align_bytes=64)
+            x_grouped[i] = keep.tile([P, len(CHUNKS[i][0]) * C, PACK], BF16, name="xg_%d" % i, tag=CHUNKS[i][1], align_bytes=64)
 
         def cast_and_gather(t):
             planes_bf[t] = keep.tile([P, T], BF16, name="plane_bf%d" % t)
@@ -106,21 +104,18 @@ def tile_routed_moe_kernel(tc, xT, w, gate, offs, pos1, pos2, out):
             for c0 in range(0, T, step):
                 caster = nc.gpsimd if CASTERS[t] == "g" else nc.vector
                 caster.tensor_copy(planes_bf[t][:, c0 : c0 + step], planes[t][:, c0 : c0 + step])
-            e0, n = CHUNKS[0][0], CHUNKS[0][1]
-            nc.vector.tensor_copy(g4[:, t, :], planes[t][:].indirect(offs_sb[:, e0 * C // 16 : (e0 + n) * C // 16]))
-
-            if t >= 2:
-                e = E - 1
-                nc.vector.tensor_copy(g2[:, t - 2, :], planes[t][:].indirect(offs_sb[:, e * C // 16 : (e + 1) * C // 16]))
+            n = V_EXPERTS if t < 2 else V_EXPERTS + 1
+            nc.vector.tensor_copy(g4[:, t, : n * C], planes[t][:].indirect(offs_sb[:, : n * C // 16]))
 
         def interleave_tokens():
             grouped_tile(0)
             nc.vector.tensor_copy(
-                x_grouped[0][:].rearrange("p (c i) t -> p c t i", i=4), g4[:].rearrange("p t (c i) -> p c t i", i=4)
+                x_grouped[0][:].rearrange("p (c i) t -> p c t i", i=4),
+                g4[:, :, : V_EXPERTS * C].rearrange("p t (c i) -> p c t i", i=4),
             )
 
         def gather_expert(i, m, t):
-            e = CHUNKS[i][0] + m
+            e = CHUNKS[i][0][m]
             nc.scalar.activation(
                 x_grouped[i][:, m * C : (m + 1) * C, t],
                 planes_bf[t][:].indirect(offs_sb[:, e * C // 16 : (e + 1) * C // 16]),
@@ -148,11 +143,11 @@ def tile_routed_moe_kernel(tc, xT, w, gate, offs, pos1, pos2, out):
             )
 
         def quantize_tokens(i):
-            n, pieces = CHUNKS[i][1], CHUNKS[i][4]
-            x_codes[i] = keep.tile([P, n * C], U32, name="xc_%d" % i, tag=CHUNKS[i][3], align_bytes=64)
+            n = len(CHUNKS[i][0])
+            x_codes[i] = keep.tile([P, n * C], U32, name="xc_%d" % i, tag=CHUNKS[i][2], align_bytes=64)
             x_scales[i] = keep.tile([P, n * C], U8, name="xs_%d" % i, align_bytes=64)
             flat = x_grouped[i][:].rearrange("p n t -> p (n t)")
-            for m0, k, cp in pieces:
+            for m0, k in CHUNKS[i][3]:
                 cols = slice(m0 * C, (m0 + k) * C)
                 nc.vector.quantize_mx(
                     out=x_codes[i][:, cols].bitcast(FP8X4),
@@ -161,11 +156,11 @@ def tile_routed_moe_kernel(tc, xT, w, gate, offs, pos1, pos2, out):
                 )
 
         def multiply(i):
-            e0, pieces = CHUNKS[i][0], CHUNKS[i][4]
-            for m0, k, cp in pieces:
+            experts = CHUNKS[i][0]
+            for m0, k, cp in CHUNKS[i][4]:
                 bank = psum.tile([P, k * C], F32, name="bank%d_%d" % (i, m0))
                 for m in range(m0, m0 + k):
-                    g, q = divmod(e0 + m, WGROUP)
+                    g, q = divmod(experts[m], WGROUP)
                     wc = slice(q * N, (q + 1) * N)
                     xc = slice(m * C, (m + 1) * C)
                     nc.tensor.matmul_mx(
@@ -177,7 +172,7 @@ def tile_routed_moe_kernel(tc, xT, w, gate, offs, pos1, pos2, out):
                         start=True,
                         stop=True,
                     )
-                dst = y[:, (e0 + m0) * C : (e0 + m0 + k) * C]
+                dst = y[:, experts[m0] * C : (experts[m0] + k) * C]
                 if cp == "s":
                     nc.scalar.copy(dst, bank[:])
                 else:
@@ -186,20 +181,18 @@ def tile_routed_moe_kernel(tc, xT, w, gate, offs, pos1, pos2, out):
         for t in range(PACK):
             cast_and_gather(t)
         interleave_weights(0)
-        for i in (1, 2):
-            grouped_tile(i)
+        grouped_tile(1)
         for t in range(PACK):
-            for i in (1, 2):
-                for m in range(CHUNKS[i][1]):
-                    gather_expert(i, m, t)
+            for m in range(8):
+                gather_expert(1, m, t)
         interleave_weights(1)
         interleave_weights(2)
         interleave_tokens()
-        grouped_tile(3)
-        for m in range(CHUNKS[3][1]):
+        grouped_tile(2)
+        for m in range(3):
             for t in range(PACK if m < 2 else 2):
-                gather_expert(3, m, t)
-        nc.vector.tensor_copy(x_grouped[3][:, 2 * C : 3 * C, 2:4], g2[:].rearrange("p t c -> p c t"))
+                gather_expert(2, m, t)
+        nc.vector.tensor_copy(x_grouped[2][:, 2 * C : 3 * C, 2:4], g4[:, 2:4, V_EXPERTS * C :].rearrange("p t c -> p c t"))
         quantize_weights(0)
         interleave_weights(4)
         quantize_tokens(0)
@@ -209,12 +202,10 @@ def tile_routed_moe_kernel(tc, xT, w, gate, offs, pos1, pos2, out):
         quantize_tokens(1)
         interleave_weights(12)
         quantize_weights(2)
+        quantize_weights(3)
         multiply(1)
         quantize_tokens(2)
-        quantize_weights(3)
         multiply(2)
-        quantize_tokens(3)
-        multiply(3)
 
         for h, (c0, c1) in enumerate(STORES):
             first = keep.tile([P, c1 - c0], F32, name="first%d" % h)

@@ -31,18 +31,18 @@ LOADS = (
     ("x", 3),
     ("w", 0, 1),
     ("w", 1, 1),
-    ("w", 2, 2),
     ("w", 4, 4),
+    ("w", 2, 2),
     ("w", 8, 4),
-    ("w", 12, 4),
+    ("w", 12, 2),
+    ("w", 14, 2),
 )
-RAW_TAGS = {0: "raw_e0", 1: "raw_e1", 2: "raw_e2", 4: "raw1", 8: "raw2", 12: "raw3"}
-WC_TAGS = ("wc0", "raw2", "raw3", "wc3")
+WC_TAGS = ("wc0", "raw8", "wc2", "wc3")
 V_EXPERTS = 5
 CHUNKS = (
-    ((0, 1, 2, 3, 4), "raw_e2", "raw1", ((0, 4), (4, 1)), ((0, 4, "s"), (4, 1, "s"))),
-    ((6, 7, 8, 9, 10, 11, 12, 13), "xg1", "wg1", ((0, 8),), ((0, 4, "s"), (4, 4, "s"))),
-    ((14, 15, 5), "raw_e1", "wg2", ((0, 2), (2, 1)), ((0, 2, "v"), (2, 1, "v"))),
+    ((0, 1, 2, 3, 4), "xg0", "raw4", ((0, 4), (4, 1)), ((0, 4, "s"), (4, 1, "s"))),
+    ((6, 7, 8, 9, 10, 11, 12, 13), "xg1", "raw12", ((0, 8),), ((0, 4, "s"), (4, 2, "s"), (6, 2, "v"))),
+    ((14, 15, 5), "raw1", "wg2", ((0, 2), (2, 1)), ((0, 2, "v"), (2, 1, "v"))),
 )
 
 
@@ -73,7 +73,7 @@ def tile_routed_moe_kernel(tc, xT, w, gate, offs, pos1, pos2, out):
                     nc.sync.dma_start(offs_sb[:], offs)
             else:
                 e, k = load[1], load[2]
-                w_raw[e] = keep.tile([P, k, PACK * N], F32, name="w_raw%d" % e, tag=RAW_TAGS[e], align_bytes=64)
+                w_raw[e] = keep.tile([P, k, PACK * N], F32, name="w_raw%d" % e, tag="raw%d" % e, align_bytes=64)
                 nc.sync.dma_start(w_raw[e][:], w_view[:, e : e + k, :])
         pos1_sb = lists.tile([P, T // 16], U16, name="pos1_sb")
         nc.sync.dma_start(pos1_sb[:], pos1)
@@ -186,21 +186,22 @@ def tile_routed_moe_kernel(tc, xT, w, gate, offs, pos1, pos2, out):
             for m in range(8):
                 gather_expert(1, m, t)
         interleave_weights(1)
-        interleave_weights(2)
         interleave_tokens()
         grouped_tile(2)
         for m in range(3):
             for t in range(PACK if m < 2 else 2):
                 gather_expert(2, m, t)
         nc.vector.tensor_copy(x_grouped[2][:, 2 * C : 3 * C, 2:4], g4[:, 2:4, V_EXPERTS * C :].rearrange("p t c -> p c t"))
-        quantize_weights(0)
         interleave_weights(4)
+        interleave_weights(2)
         quantize_tokens(0)
+        quantize_weights(0)
         interleave_weights(8)
+        interleave_weights(12)
         quantize_weights(1)
         multiply(0)
         quantize_tokens(1)
-        interleave_weights(12)
+        interleave_weights(14)
         quantize_weights(2)
         quantize_weights(3)
         multiply(1)

from contextlib import ExitStack

import concourse.mybir as mybir

K, T, E, C, N = 512, 1024, 16, 128, 128
FLOPS = 2 * K * N * E * C

F32 = mybir.dt.float32
BF16 = mybir.dt.bfloat16
U32 = mybir.dt.uint32
U16 = mybir.dt.uint16
U8 = mybir.dt.uint8
FP8X4 = mybir.dt.float8_e4m3fn_x4
MULT = mybir.AluOpType.mult
ADD = mybir.AluOpType.add
COPY = mybir.ActivationFunctionType.Copy

P = 128
PACK = 4
SLOTS = E * C
WGROUP = 4
STORES = ((0, 768), (768, 1024))

PIECES = (4, 1, 1, 1)
CASTERS = ("v", "g", "g", "g")
G_EXPERTS = 2
LOADS = (
    ("x", 0),
    ("x", 1),
    ("x", 2),
    ("x", 3),
    ("w", 0, 1),
    ("w", 1, 1),
    ("w", 4, 4),
    ("w", 2, 2),
    ("w", 8, 4),
    ("w", 12, 2),
    ("w", 14, 2),
)
WC_TAGS = ("wc0", "raw8", "wc2", "wc3")
V_EXPERTS = 5
CHUNKS = (
    ((0, 1, 2, 3, 4), "xg0", "raw4", ((0, 4), (4, 1)), ((0, 4, "s"), (4, 1, "s"))),
    ((6, 7, 8, 9, 10, 11, 12, 13), "xg1", "raw12", ((0, 8),), ((0, 4, "s"), (4, 2, "s"), (6, 2, "v"))),
    ((14, 15, 5), "raw1", "wg2", ((0, 2), (2, 1)), ((0, 2, "v"), (2, 1, "v"))),
)


def tile_routed_moe_kernel(tc, xT, w, gate, offs, pos1, pos2, out):
    nc = tc.nc
    with ExitStack() as ctx:
        lists = ctx.enter_context(tc.tile_pool(name="lists", bufs=1))
        keep = ctx.enter_context(tc.tile_pool(name="keep", bufs=1))
        psum = ctx.enter_context(tc.psum_pool(name="psum", bufs=1))

        warm = keep.tile([P, 2], F32, name="warm")
        nc.gpsimd.memset(warm[:, 0:1], 0.0)
        nc.scalar.activation(warm[:, 1:2], warm[:, 0:1], COPY)

        offs_sb = lists.tile([P, SLOTS // 16], U16, name="offs_sb")
        x_view = xT.rearrange("(p t) n -> p t n", t=PACK)
        w_view = w.rearrange("e (p j) n -> p e (j n)", j=PACK)
        planes = {}
        w_raw = {}
        for load in LOADS:
            if load[0] == "x":
                t = load[1]
                planes[t] = keep.tile([P, T], F32, name="plane%d" % t)
                step = T // PIECES[t]
                for c0 in range(0, T, step):
                    nc.sync.dma_start(planes[t][:, c0 : c0 + step], x_view[:, t, c0 : c0 + step])
                if t == 0:
                    nc.sync.dma_start(offs_sb[:], offs)
            else:
                e, k = load[1], load[2]
                w_raw[e] = keep.tile([P, k, PACK * N], F32, name="w_raw%d" % e, tag="raw%d" % e, align_bytes=64)
                nc.sync.dma_start(w_raw[e][:], w_view[:, e : e + k, :])
        pos1_sb = lists.tile([P, T // 16], U16, name="pos1_sb")
        nc.sync.dma_start(pos1_sb[:], pos1)
        pos2_sb = lists.tile([P, T // 16], U16, name="pos2_sb")
        nc.sync.dma_start(pos2_sb[:], pos2)
        gate_sb = []
        for r in range(2):
            gt = keep.tile([P, T], F32, name="gate%d" % r)
            nc.sync.dma_start(gt[:], gate[r])
            gate_sb.append(gt)

        y = keep.tile([P, SLOTS], F32, name="y")
        planes_bf = {}
        x_grouped = {}
        x_codes = {}
        x_scales = {}
        w_grouped = {}
        w_codes = {}
        w_scales = {}
        g4 = keep.tile([P, PACK, (V_EXPERTS + 1) * C], F32, name="g4")

        def grouped_tile(i):
            x_grouped[i] = keep.tile([P, len(CHUNKS[i][0]) * C, PACK], BF16, name="xg_%d" % i, tag=CHUNKS[i][1], align_bytes=64)

        def cast_and_gather(t):
            planes_bf[t] = keep.tile([P, T], BF16, name="plane_bf%d" % t)
            step = T // PIECES[t]
            for c0 in range(0, T, step):
                caster = nc.gpsimd if CASTERS[t] == "g" else nc.vector
                caster.tensor_copy(planes_bf[t][:, c0 : c0 + step], planes[t][:, c0 : c0 + step])
            n = V_EXPERTS if t < 2 else V_EXPERTS + 1
            nc.vector.tensor_copy(g4[:, t, : n * C], planes[t][:].indirect(offs_sb[:, : n * C // 16]))

        def interleave_tokens():
            grouped_tile(0)
            nc.vector.tensor_copy(
                x_grouped[0][:].rearrange("p (c i) t -> p c t i", i=4),
                g4[:, :, : V_EXPERTS * C].rearrange("p t (c i) -> p c t i", i=4),
            )

        def gather_expert(i, m, t):
            e = CHUNKS[i][0][m]
            nc.scalar.activation(
                x_grouped[i][:, m * C : (m + 1) * C, t],
                planes_bf[t][:].indirect(offs_sb[:, e * C // 16 : (e + 1) * C // 16]),
                COPY,
            )

        def interleave_weights(e):
            g, q = divmod(e, WGROUP)
            k = w_raw[e][:].shape[1]
            if g not in w_grouped:
                w_grouped[g] = keep.tile([P, WGROUP, N, PACK], BF16, name="wg_%d" % g, tag="wg%d" % g, align_bytes=64)
            if e < G_EXPERTS:
                nc.gpsimd.tensor_copy(w_grouped[g][:, q], w_raw[e][:, 0].rearrange("p (j n) -> p n j", j=PACK))
            else:
                nc.vector.tensor_copy(
                    w_grouped[g][:, q : q + k].rearrange("p e (c i) j -> p e c j i", i=4),
                    w_raw[e][:].rearrange("p e (j c i) -> p e c j i", j=PACK, i=4),
                )

        def quantize_weights(g):
            w_codes[g] = keep.tile([P, WGROUP * N], U32, name="wc_%d" % g, tag=WC_TAGS[g], align_bytes=64)
            w_scales[g] = keep.tile([P, WGROUP * N], U8, name="ws_%d" % g, align_bytes=64)
            nc.vector.quantize_mx(
                out=w_codes[g][:].bitcast(FP8X4), scales=w_scales[g][:], in_=w_grouped[g][:].rearrange("p e n j -> p (e n j)")
            )

        def quantize_tokens(i):
            n = len(CHUNKS[i][0])
            x_codes[i] = keep.tile([P, n * C], U32, name="xc_%d" % i, tag=CHUNKS[i][2], align_bytes=64)
            x_scales[i] = keep.tile([P, n * C], U8, name="xs_%d" % i, align_bytes=64)
            flat = x_grouped[i][:].rearrange("p n t -> p (n t)")
            for m0, k in CHUNKS[i][3]:
                cols = slice(m0 * C, (m0 + k) * C)
                nc.vector.quantize_mx(
                    out=x_codes[i][:, cols].bitcast(FP8X4),
                    scales=x_scales[i][:, cols],
                    in_=flat[:, m0 * C * PACK : (m0 + k) * C * PACK],
                )

        def multiply(i):
            experts = CHUNKS[i][0]
            for m0, k, cp in CHUNKS[i][4]:
                bank = psum.tile([P, k * C], F32, name="bank%d_%d" % (i, m0))
                for m in range(m0, m0 + k):
                    g, q = divmod(experts[m], WGROUP)
                    wc = slice(q * N, (q + 1) * N)
                    xc = slice(m * C, (m + 1) * C)
                    nc.tensor.matmul_mx(
                        out=bank[:, (m - m0) * C : (m - m0 + 1) * C],
                        lhsT=w_codes[g][:, wc].bitcast(FP8X4),
                        lhsT_scale=w_scales[g][:, wc],
                        rhs=x_codes[i][:, xc].bitcast(FP8X4),
                        rhs_scale=x_scales[i][:, xc],
                        start=True,
                        stop=True,
                    )
                dst = y[:, experts[m0] * C : (experts[m0] + k) * C]
                if cp == "s":
                    nc.scalar.copy(dst, bank[:])
                else:
                    nc.vector.tensor_copy(dst, bank[:])

        for t in range(PACK):
            cast_and_gather(t)
        interleave_weights(0)
        grouped_tile(1)
        for t in range(PACK):
            for m in range(8):
                gather_expert(1, m, t)
        interleave_weights(1)
        interleave_tokens()
        grouped_tile(2)
        for m in range(3):
            for t in range(PACK if m < 2 else 2):
                gather_expert(2, m, t)
        nc.vector.tensor_copy(x_grouped[2][:, 2 * C : 3 * C, 2:4], g4[:, 2:4, V_EXPERTS * C :].rearrange("p t c -> p c t"))
        interleave_weights(4)
        interleave_weights(2)
        quantize_tokens(0)
        quantize_weights(0)
        interleave_weights(8)
        interleave_weights(12)
        quantize_weights(1)
        multiply(0)
        quantize_tokens(1)
        interleave_weights(14)
        quantize_weights(2)
        quantize_weights(3)
        multiply(1)
        quantize_tokens(2)
        multiply(2)

        for h, (c0, c1) in enumerate(STORES):
            first = keep.tile([P, c1 - c0], F32, name="first%d" % h)
            nc.vector.tensor_tensor(first[:], y[:].indirect(pos1_sb[:, c0 // 16 : c1 // 16]), gate_sb[0][:, c0:c1], MULT)
            second = keep.tile([P, c1 - c0], F32, name="second%d" % h)
            nc.vector.tensor_tensor(second[:], y[:].indirect(pos2_sb[:, c0 // 16 : c1 // 16]), gate_sb[1][:, c0:c1], MULT)
            total = keep.tile([P, c1 - c0], F32, name="total%d" % h)
            nc.vector.tensor_tensor(total[:], first[:], second[:], ADD)
            nc.sync.dma_start(out[:, c0:c1], total[:])
